import numpy as np
import ml_dtypes


def mxq(x, axis, fmt="e4m3"):
    dtype, down = {"e4m3": (ml_dtypes.float8_e4m3fn, 7), "e5m2": (ml_dtypes.float8_e5m2, 14)}[fmt]
    v = np.moveaxis(np.asarray(x, np.float32).astype(ml_dtypes.bfloat16).astype(np.float64), axis, -1)
    blocks = v.reshape(v.shape[:-1] + (-1, 32))
    amax = np.abs(blocks).max(-1, keepdims=True)
    byte = np.maximum(np.where(amax > 0, np.frexp(amax)[1] - 1 + 127, 0) - down, 1)
    scale = np.exp2(byte - 127.0)
    codes = (blocks / scale).astype(np.float32).astype(dtype).astype(np.float64)
    return np.moveaxis((codes * scale).reshape(v.shape), -1, axis)


WIDE = False


def mx_kscale(k):
    if not WIDE:
        return np.ones(k)
    levels = np.array([10, -10, 5, -5, 0])
    if k % 512:
        return np.exp2(np.random.permutation(np.resize(levels, k // 32))).repeat(32)
    a = np.empty((k // 512, 16))
    for p in range(k // 512):
        a[p, :8] = np.random.permutation(np.resize(levels, 8))
        for g in range(8):
            far = levels[np.abs(levels - a[p, g]) >= 10]
            a[p, g + 8] = far[np.random.randint(len(far))]
    return np.exp2(a.ravel()).repeat(32)


def f64(x):
    return np.asarray(x).astype(np.float64)


def striped(idx):
    return np.tile(idx.reshape(-1, 16).T, (8, 1)).astype(np.uint16)


def unstriped(offs):
    return offs[:16].T.reshape(-1).astype(np.int64)


def pack_weight(w):
    k, n = w.shape
    w = f64(np.asarray(w, np.float32).astype(ml_dtypes.bfloat16)).reshape(k // 32, 32, n)
    amax = np.abs(w).max(1)
    byte = np.clip(np.where(amax > 0, np.frexp(amax)[1] - 1 + 127 - 7, 1), 1, 254)
    scaled = (w * np.exp2(127.0 - byte)[:, None, :]).reshape(k, n).astype(np.float32)
    words = np.ascontiguousarray(scaled.reshape(k // 512, 128, 4, n).transpose(0, 1, 3, 2)).astype(ml_dtypes.float8_e4m3fn).view(np.uint8)
    return words, np.ascontiguousarray(byte.astype(np.uint8).reshape(k // 512, 16, n))


def unpack_weight(words, scales):
    g, p, n, _ = words.shape
    vals = np.ascontiguousarray(words).view(ml_dtypes.float8_e4m3fn).astype(np.float64) * np.repeat(np.exp2(scales.astype(np.float64) - 127.0), 8, axis=1)[..., None]
    return vals.transpose(0, 1, 3, 2).reshape(g * 512, n)


def sigmoid(v):
    return 1.0 / (1.0 + np.exp(-np.maximum(v, -700.0)))


K, T, S, N, U = 512, 2048, 512, 256, 1024
P = 2 ** 7


def setup_inputs():
    n = np.random.standard_normal
    s = mx_kscale(K)[:, None]
    packed_xT = pack_weight(n((K, T)) * s)
    return {
        "x_words": packed_xT[0],
        "x_scales": packed_xT[1],
        "w1": (n((K, N)) / np.sqrt(K) / s).astype(np.float32),
        "w2": (n((K, N)) / np.sqrt(K) / s).astype(np.float32),
        "buf": (n((N, U))).astype(np.float32),
        "sent": (np.tile((np.random.uniform(size=S) < 0.8) * 1.0, (P, 1))).astype(np.float32),
        "lim": (np.tile(np.random.uniform(1.0, 2.5, S), (P, 1))).astype(np.float32),
        "offs": striped(np.random.permutation(T)[:S]),
        "slot": striped(np.random.permutation(U)[:S]),
    }


def reference(x_words, x_scales, w1, w2, buf, sent, lim, offs, slot):
    bufg = f64(buf)[:, unstriped(slot)]
    xq = unpack_weight(x_words, x_scales)[:, unstriped(offs)]
    yr = mxq(f64(w1), 0, "e4m3").T @ xq
    yg = mxq(f64(w2), 0, "e4m3").T @ xq
    gain = sigmoid(yg)
    llr = 2.0 * ((yr * gain) / (-1.0 * gain + 1.2))
    comb = bufg + f64(sent)[:1] * llr
    return np.log(np.exp(-1.0 * (np.abs(np.maximum(np.minimum(comb, f64(lim)[:1]), -1.0 * f64(lim)[:1])))) + 1.0) + 0.1 * ((comb - bufg) ** 2)

@@ -1,0 +1,129 @@
+import math
+from contextlib import ExitStack
+
+import concourse.mybir as mybir
+from concourse.masks import make_identity
+
+K, T, S, N, U = 512, 2048, 512, 256, 1024
+P = 128
+PACK = 4
+FLOPS = 2 * 2 * K * N * S
+
+F32 = mybir.dt.float32
+BF16 = mybir.dt.bfloat16
+I32 = mybir.dt.int32
+U32 = mybir.dt.uint32
+U16 = mybir.dt.uint16
+U8 = mybir.dt.uint8
+FP8X4 = mybir.dt.float8_e4m3fn_x4
+ACT = mybir.ActivationFunctionType
+ALU = mybir.AluOpType
+
+
+def tile_picked_yharq_doubt_p_kernel(tc, x_words, x_scales, w1, w2, buf, sent, lim, offs, slot, out):
+    nc = tc.nc
+    halves = N // P
+    with ExitStack() as ctx:
+        keep = ctx.enter_context(tc.tile_pool(name="keep", bufs=1))
+        psum = ctx.enter_context(tc.psum_pool(name="psum", bufs=1))
+
+        offs_t = keep.tile([P, S // 16], U16, name="offs_t")
+        slot_t = keep.tile([P, S // 16], U16, name="slot_t")
+        reuse = ctx.enter_context(tc.tile_pool(name="reuse", bufs=1))
+        xs_all = reuse.tile([P, T], U8, name="xs_all", offset=4096 - 1024, align_bytes=64)
+        xw = reuse.tile([P, S], U32, name="xw", offset=4096, align_bytes=64)
+        xw_all = reuse.tile([P, T], I32, name="xw_all", offset=8192, align_bytes=64)
+        w_raw = [reuse.tile([P, PACK, N], F32, name="w_raw0", offset=16384), keep.tile([P, PACK, N], F32, name="w_raw1")]
+        buf_t = [reuse.tile([P, U], F32, name="buf0", offset=16384), reuse.tile([P, U], F32, name="buf1", offset=0)]
+        sent_col = reuse.tile([P, PACK], F32, name="sent_col", offset=6144)
+        lim_col = reuse.tile([P, PACK], F32, name="lim_col", offset=6144 + 32)
+        ident = keep.tile([P, P], F32, name="ident")
+
+        nc.vector.memset(xs_all[:].bitcast(I32), 0)
+        make_identity(nc, ident[:])
+
+        nc.sync.dma_start(offs_t[:], offs)
+        nc.sync.dma_start(sent_col[:], sent[0].rearrange("(p t) -> p t", t=PACK))
+        nc.sync.dma_start(lim_col[:], lim[0].rearrange("(p t) -> p t", t=PACK))
+        for q in range(4):
+            nc.scalar.dma_start(xs_all[32 * q : 32 * q + 4, :].bitcast(I32), x_scales[0, 4 * q : 4 * q + 4, :].bitcast(I32))
+        nc.sync.dma_start(w_raw[0][:], w1.rearrange("(p j) n -> p j n", j=PACK))
+        nc.sync.dma_start(xw_all[:], x_words[0].rearrange("p n t -> p (n t)").bitcast(I32))
+        nc.sync.dma_start(w_raw[1][:], w2.rearrange("(p j) n -> p j n", j=PACK))
+        nc.sync.dma_start(slot_t[:], slot)
+
+        xs = reuse.tile([P, S], U8, name="xs", offset=6144, align_bytes=64)
+
+        sent_ps = psum.tile([P, PACK, P], F32, name="sent_ps")
+        lim_ps = psum.tile([P, PACK, P], F32, name="lim_ps")
+        for col, ps in ((sent_col, sent_ps), (lim_col, lim_ps)):
+            for t in range(PACK):
+                nc.tensor.transpose(ps[:, t, :], col[:, t : t + 1].to_broadcast([P, P]), ident[:])
+        sent5 = keep.tile([P, S], F32, name="sent5")
+        tlim = keep.tile([P, S], F32, name="tlim")
+        nc.scalar.activation(sent5[:].rearrange("q (p t) -> q p t", t=PACK), sent_ps[:].rearrange("q t p -> q p t"), ACT.Copy, scale=5.0)
+        nc.scalar.activation(tlim[:].rearrange("q (p t) -> q p t", t=PACK), lim_ps[:].rearrange("q t p -> q p t"), ACT.Tanh, scale=0.5)
+
+        def quantise(i, h, on_scalar):
+            if i == 0:
+                grouped = keep.tile([P, P, PACK], BF16, name=f"grouped{i}{h}", align_bytes=64)
+            else:
+                grouped = reuse.tile([P, P, PACK], BF16, name=f"grouped{i}{h}", offset=8192 + h * 1024, align_bytes=64)
+            src = w_raw[i][:, :, h * P : (h + 1) * P].rearrange("p t (c e) -> p c t e", e=4)
+            dst = grouped[:].rearrange("p (c e) t -> p c t e", e=4)
+            if on_scalar:
+                nc.scalar.copy(dst, src)
+            else:
+                nc.vector.tensor_copy(dst, src)
+            return grouped
+
+        def to_mx(i, h, grouped):
+            codes = keep.tile([P, P], U32, name=f"codes{i}{h}", align_bytes=64)
+            scales = keep.tile([P, P], U8, name=f"scales{i}{h}", align_bytes=64)
+            nc.vector.quantize_mx(out=codes[:].bitcast(FP8X4), scales=scales[:], in_=grouped[:].rearrange("p c t -> p (c t)"))
+            return codes, scales
+
+        def product(i, h, codes, scales):
+            acc = psum.tile([P, S], F32, name=f"y{i}{h}")
+            nc.tensor.matmul_mx(out=acc[:], lhsT=codes[:].bitcast(FP8X4), lhsT_scale=scales[:], rhs=xw[:].bitcast(FP8X4), rhs_scale=xs[:], start=True, stop=True)
+            return acc
+
+        y = {}
+        g1 = [quantise(0, h, False) for h in range(halves)]
+        q1 = [to_mx(0, h, g1[h]) for h in range(halves)]
+        nc.sync.dma_start(buf_t[0][:], buf[0:P, :])
+        nc.vector.tensor_copy(xs[:], xs_all[:].indirect(offs_t[:]))
+        nc.sync.dma_start(buf_t[1][:], buf[P : 2 * P, :])
+        nc.vector.tensor_copy(xw[:], xw_all[:].bitcast(U32).indirect(offs_t[:]))
+        for h in range(halves):
+            y[0, h] = product(0, h, *q1[h])
+        g2 = [quantise(1, h, h == 1) for h in range(halves)]
+        for h in range(halves):
+            y[1, h] = product(1, h, *to_mx(1, h, g2[h]))
+
+        def tiles(name):
+            return [keep.tile([P, S], F32, name=f"{name}{h}") for h in range(halves)]
+
+        u, g, d, c, tc_, sq, mag, clip, lg, res = (tiles(n) for n in ("u", "g", "d", "c", "tc", "sq", "mag", "clip", "lg", "res"))
+        for h in range(halves):
+            nc.vector.tensor_tensor(u[h][:], y[0, h][:], sent5[:], ALU.mult)
+        for h in range(halves):
+            nc.scalar.activation(g[h][:], y[1, h][:], ACT.Tanh, scale=0.5, bias=-0.5 * math.log(6.0))
+        for h in range(halves):
+            nc.vector.scalar_tensor_tensor(d[h][:], g[h][:], 1.0, u[h][:], ALU.add, ALU.mult)
+            nc.scalar.activation(sq[h][:], d[h][:], ACT.Square, scale=math.sqrt(0.1))
+        W = S // 2
+        for h in range(halves):
+            for j in range(2):
+                cols = slice(j * W, (j + 1) * W)
+                nc.vector.tensor_tensor(c[h][:, cols], buf_t[h][:].indirect(slot_t[:, j * W // 16 : (j + 1) * W // 16]), d[h][:, cols], ALU.add)
+                nc.scalar.activation(tc_[h][:, cols], c[h][:, cols], ACT.Tanh, scale=0.5)
+        for h in range(halves):
+            nc.vector.scalar_tensor_tensor(mag[h][:], tc_[h][:], -1.0, tc_[h][:], ALU.mult, ALU.max)
+            nc.vector.tensor_tensor(clip[h][:], mag[h][:], tlim[:], ALU.min)
+        for h in range(halves):
+            for j in range(2):
+                cols = slice(j * W, (j + 1) * W)
+                nc.scalar.activation(lg[h][:, cols], clip[h][:, cols], ACT.Ln, scale=0.5, bias=0.5)
+                nc.vector.tensor_tensor(res[h][:, cols], sq[h][:, cols], lg[h][:, cols], ALU.subtract)
+                nc.sync.dma_start(out[h * P : (h + 1) * P, cols], res[h][:, cols])

@@ -23,52 +23,44 @@ ALU = mybir.AluOpType
 def tile_picked_yharq_doubt_p_kernel(tc, x_words, x_scales, w1, w2, buf, sent, lim, offs, slot, out):
     nc = tc.nc
     halves = N // P
+    W = S // 2
     with ExitStack() as ctx:
         keep = ctx.enter_context(tc.tile_pool(name="keep", bufs=1))
+        reuse = ctx.enter_context(tc.tile_pool(name="reuse", bufs=1))
         psum = ctx.enter_context(tc.psum_pool(name="psum", bufs=1))
 
         offs_t = keep.tile([P, S // 16], U16, name="offs_t")
         slot_t = keep.tile([P, S // 16], U16, name="slot_t")
-        reuse = ctx.enter_context(tc.tile_pool(name="reuse", bufs=1))
-        xs_all = reuse.tile([P, T], U8, name="xs_all", offset=4096 - 1024, align_bytes=64)
-        xw = reuse.tile([P, S], U32, name="xw", offset=4096, align_bytes=64)
-        xw_all = reuse.tile([P, T], I32, name="xw_all", offset=8192, align_bytes=64)
-        w_raw = [reuse.tile([P, PACK, N], F32, name="w_raw0", offset=16384), keep.tile([P, PACK, N], F32, name="w_raw1")]
-        buf_t = [reuse.tile([P, U], F32, name="buf0", offset=16384), reuse.tile([P, U], F32, name="buf1", offset=0)]
-        sent_col = reuse.tile([P, PACK], F32, name="sent_col", offset=6144)
-        lim_col = reuse.tile([P, PACK], F32, name="lim_col", offset=6144 + 32)
-        ident = keep.tile([P, P], F32, name="ident")
+        xs_all = keep.tile([P, T], U8, name="xs_all", align_bytes=64)
+        xw_all = reuse.tile([P, T], I32, name="xw_all", offset=0, align_bytes=64)
+        w_raw = [keep.tile([P, PACK, N], F32, name=f"w_raw{i}") for i in range(2)]
+        buf_t = [keep.tile([P, U], F32, name="buf0"), reuse.tile([P, U], F32, name="buf1", offset=4 * T)]
+        sent_t = keep.tile([P, S], F32, name="sent_t")
+        lim_t = keep.tile([P, S], F32, name="lim_t")
+        tlim = keep.tile([P, S], F32, name="tlim")
 
         nc.vector.memset(xs_all[:].bitcast(I32), 0)
-        make_identity(nc, ident[:])
-
         nc.sync.dma_start(offs_t[:], offs)
-        nc.sync.dma_start(sent_col[:], sent[0].rearrange("(p t) -> p t", t=PACK))
-        nc.sync.dma_start(lim_col[:], lim[0].rearrange("(p t) -> p t", t=PACK))
-        for q in range(4):
-            nc.scalar.dma_start(xs_all[32 * q : 32 * q + 4, :].bitcast(I32), x_scales[0, 4 * q : 4 * q + 4, :].bitcast(I32))
         nc.sync.dma_start(w_raw[0][:], w1.rearrange("(p j) n -> p j n", j=PACK))
+        for q in range(4):
+            queue = nc.sync if q < 2 else nc.scalar
+            queue.dma_start(xs_all[32 * q : 32 * q + 4, :].bitcast(I32), x_scales[0, 4 * q : 4 * q + 4, :].bitcast(I32))
         nc.sync.dma_start(xw_all[:], x_words[0].rearrange("p n t -> p (n t)").bitcast(I32))
         nc.sync.dma_start(w_raw[1][:], w2.rearrange("(p j) n -> p j n", j=PACK))
+        nc.sync.dma_start(sent_t[:], sent)
         nc.sync.dma_start(slot_t[:], slot)
+        nc.sync.dma_start(buf_t[0][:], buf[0:P, :])
+        nc.sync.dma_start(lim_t[:], lim)
+        nc.sync.dma_start(buf_t[1][:], buf[P : 2 * P, :])
 
-        xs = reuse.tile([P, S], U8, name="xs", offset=6144, align_bytes=64)
+        xs = keep.tile([P, S], U8, name="xs", align_bytes=64)
+        xw = [keep.tile([P, W], U32, name=f"xw{j}", align_bytes=64) for j in range(2)]
 
-        sent_ps = psum.tile([P, PACK, P], F32, name="sent_ps")
-        lim_ps = psum.tile([P, PACK, P], F32, name="lim_ps")
-        for col, ps in ((sent_col, sent_ps), (lim_col, lim_ps)):
-            for t in range(PACK):
-                nc.tensor.transpose(ps[:, t, :], col[:, t : t + 1].to_broadcast([P, P]), ident[:])
-        sent5 = keep.tile([P, S], F32, name="sent5")
-        tlim = keep.tile([P, S], F32, name="tlim")
-        nc.scalar.activation(sent5[:].rearrange("q (p t) -> q p t", t=PACK), sent_ps[:].rearrange("q t p -> q p t"), ACT.Copy, scale=5.0)
-        nc.scalar.activation(tlim[:].rearrange("q (p t) -> q p t", t=PACK), lim_ps[:].rearrange("q t p -> q p t"), ACT.Tanh, scale=0.5)
-
-        def quantise(i, h, on_scalar):
-            if i == 0:
+        def interleave(i, h, on_scalar):
+            if i == 0 or on_scalar:
                 grouped = keep.tile([P, P, PACK], BF16, name=f"grouped{i}{h}", align_bytes=64)
             else:
-                grouped = reuse.tile([P, P, PACK], BF16, name=f"grouped{i}{h}", offset=8192 + h * 1024, align_bytes=64)
+                grouped = reuse.tile([P, P, PACK], BF16, name=f"grouped{i}{h}", offset=h * 1024, align_bytes=64)
             src = w_raw[i][:, :, h * P : (h + 1) * P].rearrange("p t (c e) -> p c t e", e=4)
             dst = grouped[:].rearrange("p (c e) t -> p c t e", e=4)
             if on_scalar:
@@ -78,52 +70,57 @@ def tile_picked_yharq_doubt_p_kernel(tc, x_words, x_scales, w1, w2, buf, sent, l
             return grouped
 
         def to_mx(i, h, grouped):
-            codes = keep.tile([P, P], U32, name=f"codes{i}{h}", align_bytes=64)
+            if (i, h) == (1, 1):
+                codes = reuse.tile([P, P], U32, name=f"codes{i}{h}", offset=1024, align_bytes=64)
+            else:
+                codes = keep.tile([P, P], U32, name=f"codes{i}{h}", align_bytes=64)
             scales = keep.tile([P, P], U8, name=f"scales{i}{h}", align_bytes=64)
             nc.vector.quantize_mx(out=codes[:].bitcast(FP8X4), scales=scales[:], in_=grouped[:].rearrange("p c t -> p (c t)"))
             return codes, scales
 
-        def product(i, h, codes, scales):
-            acc = psum.tile([P, S], F32, name=f"y{i}{h}")
-            nc.tensor.matmul_mx(out=acc[:], lhsT=codes[:].bitcast(FP8X4), lhsT_scale=scales[:], rhs=xw[:].bitcast(FP8X4), rhs_scale=xs[:], start=True, stop=True)
-            return acc
-
-        y = {}
-        g1 = [quantise(0, h, False) for h in range(halves)]
-        q1 = [to_mx(0, h, g1[h]) for h in range(halves)]
-        nc.sync.dma_start(buf_t[0][:], buf[0:P, :])
-        nc.vector.tensor_copy(xs[:], xs_all[:].indirect(offs_t[:]))
-        nc.sync.dma_start(buf_t[1][:], buf[P : 2 * P, :])
-        nc.vector.tensor_copy(xw[:], xw_all[:].bitcast(U32).indirect(offs_t[:]))
-        for h in range(halves):
-            y[0, h] = product(0, h, *q1[h])
-        g2 = [quantise(1, h, h == 1) for h in range(halves)]
-        for h in range(halves):
-            y[1, h] = product(1, h, *to_mx(1, h, g2[h]))
+        def product(acc, mx, j):
+            nc.tensor.matmul_mx(out=acc, lhsT=mx[0][:].bitcast(FP8X4), lhsT_scale=mx[1][:], rhs=xw[j][:].bitcast(FP8X4), rhs_scale=xs[:, j * W : (j + 1) * W], start=True, stop=True)
 
         def tiles(name):
             return [keep.tile([P, S], F32, name=f"{name}{h}") for h in range(halves)]
 
-        u, g, d, c, tc_, sq, mag, clip, lg, res = (tiles(n) for n in ("u", "g", "d", "c", "tc", "sq", "mag", "clip", "lg", "res"))
-        for h in range(halves):
-            nc.vector.tensor_tensor(u[h][:], y[0, h][:], sent5[:], ALU.mult)
-        for h in range(halves):
-            nc.scalar.activation(g[h][:], y[1, h][:], ACT.Tanh, scale=0.5, bias=-0.5 * math.log(6.0))
-        for h in range(halves):
-            nc.vector.scalar_tensor_tensor(d[h][:], g[h][:], 1.0, u[h][:], ALU.add, ALU.mult)
-            nc.scalar.activation(sq[h][:], d[h][:], ACT.Square, scale=math.sqrt(0.1))
-        W = S // 2
+        u, g, d, c, tc_, sq, clip, lg, res = (tiles(n) for n in ("u", "g", "d", "c", "tc", "sq", "clip", "lg", "res"))
+        cols = [slice(j * W, (j + 1) * W) for j in range(2)]
+        yr = [psum.tile([P, S], F32, name=f"yr{h}") for h in range(halves)]
+        yg = {(h, j): psum.tile([P, W], F32, name=f"yg{h}{j}") for h in range(halves) for j in range(2)}
+        g1 = [interleave(0, h, h == 1) for h in range(halves)]
+        q1 = [to_mx(0, h, g1[h]) for h in range(halves)]
+        nc.vector.tensor_copy(xs[:], xs_all[:].indirect(offs_t[:]))
+        for j in range(2):
+            nc.vector.tensor_copy(xw[j][:], xw_all[:].bitcast(U32).indirect(offs_t[:, j * W // 16 : (j + 1) * W // 16]))
         for h in range(halves):
             for j in range(2):
-                cols = slice(j * W, (j + 1) * W)
-                nc.vector.tensor_tensor(c[h][:, cols], buf_t[h][:].indirect(slot_t[:, j * W // 16 : (j + 1) * W // 16]), d[h][:, cols], ALU.add)
-                nc.scalar.activation(tc_[h][:, cols], c[h][:, cols], ACT.Tanh, scale=0.5)
+                product(yr[h][:, cols[j]], q1[h], j)
+        g2 = [interleave(1, h, h == 1) for h in range(halves)]
+        nc.vector.scalar_tensor_tensor(u[0][:], yr[0][:], 5.0, sent_t[:], ALU.mult, ALU.mult)
+        q2 = [to_mx(1, h, g2[h]) for h in range(halves)]
+        for h in range(halves):
+            for j in range(2):
+                product(yg[h, j][:], q2[h], j)
+                nc.scalar.activation(g[h][:, cols[j]], yg[h, j][:], ACT.Tanh, scale=0.5, bias=-0.5 * math.log(6.0))
+        nc.vector.scalar_tensor_tensor(u[1][:], yr[1][:], 5.0, sent_t[:], ALU.mult, ALU.mult)
+        whole = [slice(0, S)]
+        for h in range(halves):
+            for s in (cols if h == 0 else whole):
+                nc.vector.scalar_tensor_tensor(d[h][:, s], g[h][:, s], 1.0, u[h][:, s], ALU.add, ALU.mult)
+            nc.scalar.activation(sq[h][:], d[h][:], ACT.Square, scale=math.sqrt(0.1))
+            if h == 0:
+                nc.scalar.activation(tlim[:], lim_t[:], ACT.Tanh, scale=0.5)
+            for s in (whole if h == 0 else cols):
+                nc.vector.tensor_tensor(c[h][:, s], buf_t[h][:].indirect(slot_t[:, s.start // 16 : s.stop // 16]), d[h][:, s], ALU.add)
+                nc.scalar.activation(tc_[h][:, s], c[h][:, s], ACT.Tanh, scale=0.5)
+        mag = [reuse.tile([P, S], F32, name=f"mag{h}", offset=4 * T + h * 4 * S) for h in range(halves)]
         for h in range(halves):
             nc.vector.scalar_tensor_tensor(mag[h][:], tc_[h][:], -1.0, tc_[h][:], ALU.mult, ALU.max)
+        for h in range(halves):
             nc.vector.tensor_tensor(clip[h][:], mag[h][:], tlim[:], ALU.min)
         for h in range(halves):
-            for j in range(2):
-                cols = slice(j * W, (j + 1) * W)
-                nc.scalar.activation(lg[h][:, cols], clip[h][:, cols], ACT.Ln, scale=0.5, bias=0.5)
-                nc.vector.tensor_tensor(res[h][:, cols], sq[h][:, cols], lg[h][:, cols], ALU.subtract)
-                nc.sync.dma_start(out[h * P : (h + 1) * P, cols], res[h][:, cols])
+            for s in cols:
+                nc.scalar.activation(lg[h][:, s], clip[h][:, s], ACT.Ln, scale=0.5, bias=0.5)
+                nc.vector.tensor_tensor(res[h][:, s], sq[h][:, s], lg[h][:, s], ALU.subtract)
+                nc.sync.dma_start(out[h * P : (h + 1) * P, s], res[h][:, s])

import math
from contextlib import ExitStack

import concourse.mybir as mybir
from concourse.masks import make_identity

K, T, S, N, U = 512, 2048, 512, 256, 1024
P = 128
PACK = 4
FLOPS = 2 * 2 * K * N * S

F32 = mybir.dt.float32
BF16 = mybir.dt.bfloat16
I32 = mybir.dt.int32
U32 = mybir.dt.uint32
U16 = mybir.dt.uint16
U8 = mybir.dt.uint8
FP8X4 = mybir.dt.float8_e4m3fn_x4
ACT = mybir.ActivationFunctionType
ALU = mybir.AluOpType


def tile_picked_yharq_doubt_p_kernel(tc, x_words, x_scales, w1, w2, buf, sent, lim, offs, slot, out):
    nc = tc.nc
    halves = N // P
    W = S // 2
    with ExitStack() as ctx:
        keep = ctx.enter_context(tc.tile_pool(name="keep", bufs=1))
        reuse = ctx.enter_context(tc.tile_pool(name="reuse", bufs=1))
        psum = ctx.enter_context(tc.psum_pool(name="psum", bufs=1))

        offs_t = keep.tile([P, S // 16], U16, name="offs_t")
        slot_t = keep.tile([P, S // 16], U16, name="slot_t")
        xs_all = keep.tile([P, T], U8, name="xs_all", align_bytes=64)
        xw_all = reuse.tile([P, T], I32, name="xw_all", offset=0, align_bytes=64)
        w_raw = [keep.tile([P, PACK, N], F32, name=f"w_raw{i}") for i in range(2)]
        buf_t = [keep.tile([P, U], F32, name="buf0"), reuse.tile([P, U], F32, name="buf1", offset=4 * T)]
        sent_t = keep.tile([P, S], F32, name="sent_t")
        lim_t = keep.tile([P, S], F32, name="lim_t")
        tlim = keep.tile([P, S], F32, name="tlim")

        nc.vector.memset(xs_all[:].bitcast(I32), 0)
        nc.sync.dma_start(offs_t[:], offs)
        nc.sync.dma_start(w_raw[0][:], w1.rearrange("(p j) n -> p j n", j=PACK))
        for q in range(4):
            queue = nc.sync if q < 2 else nc.scalar
            queue.dma_start(xs_all[32 * q : 32 * q + 4, :].bitcast(I32), x_scales[0, 4 * q : 4 * q + 4, :].bitcast(I32))
        nc.sync.dma_start(xw_all[:], x_words[0].rearrange("p n t -> p (n t)").bitcast(I32))
        nc.sync.dma_start(w_raw[1][:], w2.rearrange("(p j) n -> p j n", j=PACK))
        nc.sync.dma_start(sent_t[:], sent)
        nc.sync.dma_start(slot_t[:], slot)
        nc.sync.dma_start(buf_t[0][:], buf[0:P, :])
        nc.sync.dma_start(lim_t[:], lim)
        nc.sync.dma_start(buf_t[1][:], buf[P : 2 * P, :])

        xs = keep.tile([P, S], U8, name="xs", align_bytes=64)
        xw = [keep.tile([P, W], U32, name=f"xw{j}", align_bytes=64) for j in range(2)]

        def interleave(i, h, on_scalar):
            if i == 0 or on_scalar:
                grouped = keep.tile([P, P, PACK], BF16, name=f"grouped{i}{h}", align_bytes=64)
            else:
                grouped = reuse.tile([P, P, PACK], BF16, name=f"grouped{i}{h}", offset=h * 1024, align_bytes=64)
            src = w_raw[i][:, :, h * P : (h + 1) * P].rearrange("p t (c e) -> p c t e", e=4)
            dst = grouped[:].rearrange("p (c e) t -> p c t e", e=4)
            if on_scalar:
                nc.scalar.copy(dst, src)
            else:
                nc.vector.tensor_copy(dst, src)
            return grouped

        def to_mx(i, h, grouped):
            if (i, h) == (1, 1):
                codes = reuse.tile([P, P], U32, name=f"codes{i}{h}", offset=1024, align_bytes=64)
            else:
                codes = keep.tile([P, P], U32, name=f"codes{i}{h}", align_bytes=64)
            scales = keep.tile([P, P], U8, name=f"scales{i}{h}", align_bytes=64)
            nc.vector.quantize_mx(out=codes[:].bitcast(FP8X4), scales=scales[:], in_=grouped[:].rearrange("p c t -> p (c t)"))
            return codes, scales

        def product(acc, mx, j):
            nc.tensor.matmul_mx(out=acc, lhsT=mx[0][:].bitcast(FP8X4), lhsT_scale=mx[1][:], rhs=xw[j][:].bitcast(FP8X4), rhs_scale=xs[:, j * W : (j + 1) * W], start=True, stop=True)

        def tiles(name):
            return [keep.tile([P, S], F32, name=f"{name}{h}") for h in range(halves)]

        u, g, d, c, tc_, sq, clip, lg, res = (tiles(n) for n in ("u", "g", "d", "c", "tc", "sq", "clip", "lg", "res"))
        cols = [slice(j * W, (j + 1) * W) for j in range(2)]
        yr = [psum.tile([P, S], F32, name=f"yr{h}") for h in range(halves)]
        yg = {(h, j): psum.tile([P, W], F32, name=f"yg{h}{j}") for h in range(halves) for j in range(2)}
        g1 = [interleave(0, h, h == 1) for h in range(halves)]
        q1 = [to_mx(0, h, g1[h]) for h in range(halves)]
        nc.vector.tensor_copy(xs[:], xs_all[:].indirect(offs_t[:]))
        for j in range(2):
            nc.vector.tensor_copy(xw[j][:], xw_all[:].bitcast(U32).indirect(offs_t[:, j * W // 16 : (j + 1) * W // 16]))
        for h in range(halves):
            for j in range(2):
                product(yr[h][:, cols[j]], q1[h], j)
        g2 = [interleave(1, h, h == 1) for h in range(halves)]
        nc.vector.scalar_tensor_tensor(u[0][:], yr[0][:], 5.0, sent_t[:], ALU.mult, ALU.mult)
        q2 = [to_mx(1, h, g2[h]) for h in range(halves)]
        for h in range(halves):
            for j in range(2):
                product(yg[h, j][:], q2[h], j)
                nc.scalar.activation(g[h][:, cols[j]], yg[h, j][:], ACT.Tanh, scale=0.5, bias=-0.5 * math.log(6.0))
        nc.vector.scalar_tensor_tensor(u[1][:], yr[1][:], 5.0, sent_t[:], ALU.mult, ALU.mult)
        whole = [slice(0, S)]
        for h in range(halves):
            for s in (cols if h == 0 else whole):
                nc.vector.scalar_tensor_tensor(d[h][:, s], g[h][:, s], 1.0, u[h][:, s], ALU.add, ALU.mult)
            nc.scalar.activation(sq[h][:], d[h][:], ACT.Square, scale=math.sqrt(0.1))
            if h == 0:
                nc.scalar.activation(tlim[:], lim_t[:], ACT.Tanh, scale=0.5)
            for s in (whole if h == 0 else cols):
                nc.vector.tensor_tensor(c[h][:, s], buf_t[h][:].indirect(slot_t[:, s.start // 16 : s.stop // 16]), d[h][:, s], ALU.add)
                nc.scalar.activation(tc_[h][:, s], c[h][:, s], ACT.Tanh, scale=0.5)
        mag = [reuse.tile([P, S], F32, name=f"mag{h}", offset=4 * T + h * 4 * S) for h in range(halves)]
        for h in range(halves):
            nc.vector.scalar_tensor_tensor(mag[h][:], tc_[h][:], -1.0, tc_[h][:], ALU.mult, ALU.max)
        for h in range(halves):
            nc.vector.tensor_tensor(clip[h][:], mag[h][:], tlim[:], ALU.min)
        for h in range(halves):
            for s in cols:
                nc.scalar.activation(lg[h][:, s], clip[h][:, s], ACT.Ln, scale=0.5, bias=0.5)
                nc.vector.tensor_tensor(res[h][:, s], sq[h][:, s], lg[h][:, s], ALU.subtract)
                nc.sync.dma_start(out[h * P : (h + 1) * P, s], res[h][:, s])
